import numpy as np
import ml_dtypes


def mxq(x, axis, fmt="e4m3"):
    dtype, down = {"e4m3": (ml_dtypes.float8_e4m3fn, 7), "e5m2": (ml_dtypes.float8_e5m2, 14)}[fmt]
    v = np.moveaxis(np.asarray(x, np.float32).astype(ml_dtypes.bfloat16).astype(np.float64), axis, -1)
    blocks = v.reshape(v.shape[:-1] + (-1, 32))
    amax = np.abs(blocks).max(-1, keepdims=True)
    byte = np.maximum(np.where(amax > 0, np.frexp(amax)[1] - 1 + 127, 0) - down, 1)
    scale = np.exp2(byte - 127.0)
    codes = (blocks / scale).astype(np.float32).astype(dtype).astype(np.float64)
    return np.moveaxis((codes * scale).reshape(v.shape), -1, axis)


WIDE = False


def mx_kscale(k):
    if not WIDE:
        return np.ones(k)
    levels = np.array([10, -10, 5, -5, 0])
    if k % 512:
        return np.exp2(np.random.permutation(np.resize(levels, k // 32))).repeat(32)
    a = np.empty((k // 512, 16))
    for p in range(k // 512):
        a[p, :8] = np.random.permutation(np.resize(levels, 8))
        for g in range(8):
            far = levels[np.abs(levels - a[p, g]) >= 10]
            a[p, g + 8] = far[np.random.randint(len(far))]
    return np.exp2(a.ravel()).repeat(32)


def f64(x):
    return np.asarray(x).astype(np.float64)


def striped(idx):
    return np.tile(idx.reshape(-1, 16).T, (8, 1)).astype(np.uint16)


def unstriped(offs):
    return offs[:16].T.reshape(-1).astype(np.int64)


E2M1 = np.array([0.0, 0.5, 1.0, 1.5, 2.0, 3.0, 4.0, 6.0, -0.0, -0.5, -1.0, -1.5, -2.0, -3.0, -4.0, -6.0])


def pack_weight(w, fmt):
    k, n = w.shape
    w = f64(np.asarray(w, np.float32).astype(ml_dtypes.bfloat16)).reshape(k // 32, 32, n)
    amax = np.abs(w).max(1)
    if fmt == "e4m3":
        byte = np.frexp(amax)[1] - 1 + 127 - 7
    else:
        mant, ex = np.frexp(amax / 6.0)
        byte = np.where(mant > 0.5, ex, ex - 1) + 127
    byte = np.clip(np.where(amax > 0, byte, 1), 1, 254)
    scaled = (w * np.exp2(127.0 - byte)[:, None, :]).reshape(k, n).astype(np.float32)
    by_word = np.ascontiguousarray(scaled.reshape(k // 512, 128, 4, n).transpose(0, 1, 3, 2))
    if fmt == "e4m3":
        words = by_word.astype(ml_dtypes.float8_e4m3fn).view(np.uint8)
    else:
        c = by_word.astype(ml_dtypes.float4_e2m1fn).view(np.uint8) & 0xF
        words = (c[..., 0::2] | (c[..., 1::2] << 4)).reshape(k // 512, 128, 2 * n)
    return np.ascontiguousarray(words), np.ascontiguousarray(byte.astype(np.uint8).reshape(k // 512, 16, n))


def unpack_weight(words, scales, fmt):
    g, _, n = scales.shape
    words = np.ascontiguousarray(words).reshape(g, 128, n, -1)
    if fmt == "e4m3":
        vals = words.view(ml_dtypes.float8_e4m3fn).astype(np.float64)
    else:
        nib = np.empty((g, 128, n, 4), np.uint8)
        nib[..., 0::2] = words & 0xF
        nib[..., 1::2] = words >> 4
        vals = E2M1[nib]
    vals = vals * np.repeat(np.exp2(scales.astype(np.float64) - 127.0), 8, axis=1)[..., None]
    return vals.transpose(0, 1, 3, 2).reshape(g * 512, n)


def gelu(v):
    return 0.5 * v * (1.0 + np.tanh(np.sqrt(2.0 / np.pi) * (v + 0.044715 * v**3)))


K, T, S, H, T3, S2 = 1024, 2048, 512, 1024, 1024, 512

def setup_inputs():
    n = np.random.standard_normal
    s = mx_kscale(K)[:, None]
    u = mx_kscale(H)[:, None]
    tab_words, tab_scales = pack_weight(n((K, T)) * s, "e4m3")
    tab2_words, tab2_scales = pack_weight(n((H, T3)) / np.sqrt(H) / u, "e4m3")
    tab3_words, tab3_scales = pack_weight(n((H, T3)) / np.sqrt(H) / u, "e4m3")
    w4_words, w4_scales = pack_weight(1.5 * n((K, H)) / np.sqrt(K) / s, "e2m1")
    return {
        "tab_words": tab_words, "tab_scales": tab_scales,
        "offs": striped(np.random.permutation(T)[:S]),
        "tab2_words": tab2_words, "tab2_scales": tab2_scales,
        "offs2": striped(np.random.permutation(T3)[:S2]),
        "tab3_words": tab3_words, "tab3_scales": tab3_scales,
        "offs3": striped(np.random.permutation(T3)[:S2]),
        "w1": (1.5 * n((K, H)) / np.sqrt(K) / s).astype(np.float32),
        "w4_words": w4_words, "w4_scales": w4_scales,
        "gain2": (np.exp(0.3 * n(H)) * u[:, 0]).astype(np.float32),
        "gain3": (np.exp(0.3 * n(H)) * u[:, 0]).astype(np.float32),
        "d": n(S2).astype(np.float32),
    }

def reference(tab_words, tab_scales, offs, tab2_words, tab2_scales, offs2, tab3_words, tab3_scales, offs3,
              w1, w4_words, w4_scales, gain2, gain3, d):
    v = unpack_weight(tab_words, tab_scales, "e4m3")[:, unstriped(offs)]
    v2 = unpack_weight(tab2_words, tab2_scales, "e4m3")[:, unstriped(offs2)]
    v3 = unpack_weight(tab3_words, tab3_scales, "e4m3")[:, unstriped(offs3)]
    w4 = unpack_weight(w4_words, w4_scales, "e2m1")
    y1 = mxq(f64(w1), 0, "e4m3").T @ v
    y2 = w4.T @ v
    h2 = f64(gain2)[:, None] * (y1 / (1.0 + np.exp(-y1)))
    h3 = f64(gain3)[:, None] * np.maximum(y1, y2)
    e2 = v2.T @ mxq(h2, 0, "e4m3")
    e3 = v3.T @ mxq(h3, 0, "e4m3")
    out = np.tanh(e2) * (e3 + f64(d)[:, None])
    return out

@@ -1,0 +1,259 @@
+from contextlib import ExitStack
+
+import concourse.mybir as mybir
+
+K, T, S, H, T3, S2 = 1024, 2048, 512, 1024, 1024, 512
+FLOPS = 2 * (2 * K * H * S + 2 * H * S2 * S)
+
+F32 = mybir.dt.float32
+BF16 = mybir.dt.bfloat16
+I32 = mybir.dt.int32
+U32 = mybir.dt.uint32
+U16 = mybir.dt.uint16
+U8 = mybir.dt.uint8
+FP8X4 = mybir.dt.float8_e4m3fn_x4
+FP4X4 = mybir.dt.float4_e2m1fn_x4
+ACT = mybir.ActivationFunctionType
+ALU = mybir.AluOpType
+
+P = 128
+PACK = 4
+PASS = P * PACK
+PASSES = K // PASS
+BLOCKS = H // PASS
+JT = 128
+NJ = S // JT
+MT = S2 // P
+QUADS = 4
+V_SHARE = {(0, 0): 0, (1, 0): 64, (0, 1): 0, (1, 1): 0}
+GAIN2_ON_SCALAR = [(1, 0), (1, 1), (1, 2), (1, 3)]
+
+
+def tile_list_crew_staffing_score_kernel(
+    tc, tab_words, tab_scales, offs, tab2_words, tab2_scales, offs2, tab3_words, tab3_scales, offs3,
+    w1, w4_words, w4_scales, gain2, gain3, d, out,
+):
+    nc = tc.nc
+    with ExitStack() as ctx:
+        lists = ctx.enter_context(tc.tile_pool(name="lists", bufs=1))
+        keep = ctx.enter_context(tc.tile_pool(name="keep", bufs=1))
+        ring = ctx.enter_context(tc.tile_pool(name="ring", bufs=3))
+        psum = ctx.enter_context(tc.psum_pool(name="psum", bufs=8))
+
+        def held(name, shape, dtype):
+            return keep.tile(shape, dtype, name=name, align_bytes=64)
+
+        def load_list(name, src):
+            tile = lists.tile([P, 32], U16, name=name)
+            nc.sync.dma_start(tile[:], src)
+            return tile
+
+        def load_words(name, src, cols):
+            tile = held(name, [P, cols], U32)
+            nc.sync.dma_start(tile[:].bitcast(I32), src.rearrange("p n i -> p (n i)").bitcast(I32))
+            return tile
+
+        def load_both_passes(name, src):
+            tile = held(name, [P, BLOCKS * T3], U32)
+            nc.sync.dma_start(
+                tile[:].bitcast(I32).rearrange("p (a n) -> p a n", a=BLOCKS),
+                src.rearrange("a p n i -> p a (n i)").bitcast(I32),
+            )
+            return [tile[:, a * T3 : (a + 1) * T3] for a in range(BLOCKS)]
+
+        def zeroed_bytes(engine, name, cols):
+            tile = held(name, [P, cols], U8)
+            engine.memset(tile[:].bitcast(I32), 0)
+            return tile
+
+        def load_planes_side_by_side(queue, tile, scales):
+            for q in range(QUADS):
+                queue.dma_start(
+                    tile[32 * q : 32 * q + 4, :].bitcast(I32).rearrange("r (a n) -> r a n", a=PASSES),
+                    scales[:, 4 * q : 4 * q + 4, :].bitcast(I32).rearrange("a r n -> r a n"),
+                )
+
+        def load_planes_stacked(queue, tile, scales):
+            for q in range(QUADS):
+                queue.dma_start(
+                    tile[32 * q : 32 * q + 8, :].bitcast(I32),
+                    scales[:, 4 * q : 4 * q + 4, :].bitcast(I32),
+                )
+
+        def gather(name, window, offsets, dtype):
+            tile = held(name, [P, S], dtype)
+            nc.vector.tensor_copy(tile[:], window.indirect(offsets[:]))
+            return tile
+
+        def load_w1(a, b):
+            tile = held("w1_raw_%d%d" % (a, b), [P, PACK, PASS], F32)
+            rows = w1[a * PASS : (a + 1) * PASS, b * PASS : (b + 1) * PASS]
+            nc.sync.dma_start(tile[:], rows.rearrange("(p i) c -> p i c", i=PACK))
+            return tile
+
+        tab_s = zeroed_bytes(nc.vector, "tab_s", PASSES * T)
+        w4_s = zeroed_bytes(nc.vector, "w4_s", PASSES * H)
+        tab2_s = zeroed_bytes(nc.vector, "tab2_s", T3)
+        tab3_s = zeroed_bytes(nc.vector, "tab3_s", T3)
+
+        idx = load_list("idx", offs)
+        tab_w = [load_words("tab_w0", tab_words[0], T)]
+        load_planes_side_by_side(nc.sync, tab_s, tab_scales)
+        w4_w = held("w4_w", [P, PASSES * H], U16)
+        nc.sync.dma_start(
+            w4_w[:].bitcast(I32).rearrange("p (a n) -> p a n", a=PASSES),
+            w4_words.bitcast(I32).rearrange("a p n -> p a n"),
+        )
+        tab_w.append(load_words("tab_w1", tab_words[1], T))
+        load_planes_side_by_side(nc.sync, w4_s, w4_scales)
+        idx2 = load_list("idx2", offs2)
+        tab2_w = load_both_passes("tab2_w", tab2_words)
+        idx3 = load_list("idx3", offs3)
+        tab3_w = load_both_passes("tab3_w", tab3_words)
+        w1_raw = {}
+        load_planes_stacked(nc.sync, tab2_s, tab2_scales)
+        w1_raw[0, 0] = load_w1(0, 0)
+        load_planes_stacked(nc.sync, tab3_s, tab3_scales)
+        w1_raw[1, 0] = load_w1(1, 0)
+        w1_raw[0, 1] = load_w1(0, 1)
+        w1_raw[1, 1] = load_w1(1, 1)
+        g2 = held("g2", [P, BLOCKS, PACK], F32)
+        g3 = held("g3", [P, BLOCKS, PACK], F32)
+        d_sb = held("d_sb", [P, MT], F32)
+        nc.gpsimd.dma_start(g2[:], gain2.rearrange("(b p t) -> p b t", p=P, t=PACK))
+        nc.gpsimd.dma_start(g3[:], gain3.rearrange("(b p t) -> p b t", p=P, t=PACK))
+        with nc.allow_non_contiguous_dma(reason="one value of d for each partition and row tile"):
+            nc.gpsimd.dma_start(d_sb[:], d.rearrange("(mt p) -> p mt", p=P))
+
+        v_w = [gather("v_w0", tab_w[0][:], idx, U32)]
+        v_s = [gather("v_s%d" % a, tab_s[:, a * T : (a + 1) * T], idx, U8) for a in range(PASSES)]
+        w4q_w = held("w4q_w", [P, PASSES * H], U16)
+        w4q_s = held("w4q_s", [P, PASSES * H], U8)
+        deal_out, deal_in = "p (g t m) -> p g t m", "p (g m t) -> p g t m"
+        nc.scalar.copy(w4q_w[:].rearrange(deal_out, t=PACK, m=P), w4_w[:].rearrange(deal_in, t=PACK, m=P))
+        nc.vector.tensor_copy(w4q_s[:].rearrange(deal_out, t=PACK, m=P), w4_s[:].rearrange(deal_in, t=PACK, m=P))
+        v_w.append(gather("v_w1", tab_w[1][:], idx, U32))
+
+        def product(bank, lhs, rhs):
+            for a in range(2):
+                for t in range(4):
+                    lw, ls = lhs(a, t)
+                    rw, rs = rhs(a)
+                    nc.tensor.matmul_mx(
+                        out=bank[:, t, :], lhsT=lw, lhsT_scale=ls, rhs=rw, rhs_scale=rs,
+                        start=(a == 0 and t == 0), stop=(a == 1 and t == 3),
+                    )
+
+        def v_cols(jq):
+            cols = slice(jq * JT, (jq + 1) * JT)
+            return lambda a: (v_w[a][:, cols].bitcast(FP8X4), v_s[a][:, cols])
+
+        interleaved = "p t j -> p j t"
+
+        y2 = {}
+
+        def second_product(b):
+            for jq in range(NJ):
+                def w4_cols(a, t):
+                    c0 = a * H + b * PASS + t * P
+                    return w4q_w[:, c0 : c0 + P].bitcast(FP4X4), w4q_s[:, c0 : c0 + P]
+
+                bank = psum.tile([P, PACK, JT], F32, name="ybank")
+                product(bank, w4_cols, v_cols(jq))
+                y2[b, jq] = held("y2_%d%d" % (b, jq), [P, JT, PACK], F32)
+                nc.scalar.copy(y2[b, jq][:], bank[:].rearrange(interleaved))
+
+        second_product(0)
+        v2_w = [gather("v2_w%d" % a, tab2_w[a], idx2, U32) for a in range(BLOCKS)]
+        v2_s = gather("v2_s", tab2_s[:], idx2, U8)
+
+        w1q_w, w1q_s = {}, {}
+
+        def quantise_w1(a, b):
+            grouped = held("w1_bf_%d%d" % (a, b), [P, PASS * PACK], BF16)
+            dst = grouped[:].rearrange("p (t m i) -> p m i t", t=PACK, i=PACK)
+            src = w1_raw[a, b][:].rearrange("p i (m t) -> p m i t", t=PACK)
+            cut = V_SHARE[a, b]
+            if cut > 0:
+                nc.vector.tensor_copy(dst[:, :cut], src[:, :cut])
+            if cut < P:
+                nc.scalar.copy(dst[:, cut:], src[:, cut:])
+            w1q_w[a, b] = held("w1q_w%d%d" % (a, b), [P, PASS], U32)
+            w1q_s[a, b] = held("w1q_s%d%d" % (a, b), [P, PASS], U8)
+            nc.vector.quantize_mx(w1q_w[a, b][:].bitcast(FP8X4), w1q_s[a, b][:], grouped[:])
+
+        hq_w, hq_s = {}, {}
+
+        def unit(b, jq):
+            def w1_cols(a, t):
+                cols = slice(t * P, (t + 1) * P)
+                return w1q_w[a, b][:, cols].bitcast(FP8X4), w1q_s[a, b][:, cols]
+
+            bank = psum.tile([P, PACK, JT], F32, name="ybank")
+            product(bank, w1_cols, v_cols(jq))
+            y1 = bank[:].rearrange(interleaved)
+            larger = ring.tile([P, JT, PACK], F32, name="larger")
+            h = ring.tile([P, 2, JT, PACK], BF16, name="h", align_bytes=64)
+            silu = ring.tile([P, PACK * JT], F32, name="silu")
+            if (b, jq) in GAIN2_ON_SCALAR:
+                h2 = ring.tile([P, PACK, JT], BF16, name="h2")
+                nc.scalar.activation(silu[:], bank[:].rearrange("p t j -> p (t j)"), ACT.Silu)
+                for t in range(PACK):
+                    nc.scalar.activation(
+                        h2[:, t, :], silu[:, t * JT : (t + 1) * JT], ACT.Copy, scale=g2[:, b, t : t + 1]
+                    )
+            else:
+                silu_jt = silu[:].rearrange("p (j t) -> p j t", t=PACK)
+                nc.scalar.activation(silu_jt, y1, ACT.Silu)
+            nc.vector.tensor_tensor(larger[:], y1, y2[b, jq][:], ALU.max)
+            if (b, jq) not in GAIN2_ON_SCALAR:
+                nc.vector.tensor_tensor(h[:, 0], silu_jt, g2[:, b : b + 1, :].to_broadcast([P, JT, PACK]), ALU.mult)
+            nc.vector.tensor_tensor(h[:, 1], larger[:], g3[:, b : b + 1, :].to_broadcast([P, JT, PACK]), ALU.mult)
+            if (b, jq) in GAIN2_ON_SCALAR:
+                nc.vector.tensor_copy(
+                    h[:, 0].rearrange("p (c i) t -> p c t i", i=4), h2[:].rearrange("p t (c i) -> p c t i", i=4)
+                )
+            hq_w[b, jq] = held("hq_w%d%d" % (b, jq), [P, 2 * JT], U32)
+            hq_s[b, jq] = held("hq_s%d%d" % (b, jq), [P, 2 * JT], U8)
+            nc.vector.quantize_mx(
+                hq_w[b, jq][:].bitcast(FP8X4), hq_s[b, jq][:], h[:].rearrange("p e j t -> p (e j t)")
+            )
+
+        def scores(jq):
+            def cand(words, planes):
+                return lambda a, mt: (
+                    words[a][:, mt * P : (mt + 1) * P].bitcast(FP8X4),
+                    planes[4 * a : P, mt * P : (mt + 1) * P],
+                )
+
+            def h_cols(e):
+                cols = slice(e * JT, (e + 1) * JT)
+                return lambda a: (hq_w[a, jq][:, cols].bitcast(FP8X4), hq_s[a, jq][:, cols])
+
+            e2 = psum.tile([P, MT, JT], F32, name="ybank")
+            e3 = psum.tile([P, MT, JT], F32, name="ybank")
+            product(e2, cand(v2_w, v2_s), h_cols(0))
+            product(e3, cand(v3_w, v3_s), h_cols(1))
+            th = ring.tile([P, MT, JT], F32, name="th")
+            res = ring.tile([P, MT, JT], F32, name="res")
+            nc.scalar.activation(th[:], e2[:], ACT.Tanh)
+            for mt in range(MT):
+                nc.vector.scalar_tensor_tensor(
+                    res[:, mt, :], e3[:, mt, :], d_sb[:, mt : mt + 1], th[:, mt, :], ALU.add, ALU.mult
+                )
+            nc.sync.dma_start(out[:, jq * JT : (jq + 1) * JT].rearrange("(mt p) j -> p mt j", p=P), res[:])
+
+        for a in range(PASSES):
+            quantise_w1(a, 0)
+        second_product(1)
+        v3_w = [gather("v3_w%d" % a, tab3_w[a], idx3, U32) for a in range(BLOCKS)]
+        v3_s = gather("v3_s", tab3_s[:], idx3, U8)
+        for jq in range(NJ):
+            unit(0, jq)
+            if jq % 2 == 1:
+                quantise_w1(jq // 2, 1)
+        for jq in range(NJ):
+            unit(1, jq)
+            if jq > 0:
+                scores(jq - 1)
+        scores(NJ - 1)

@@ -25,7 +25,8 @@ JT = 128
 NJ = S // JT
 MT = S2 // P
 QUADS = 4
-V_SHARE = {(0, 0): 0, (1, 0): 64, (0, 1): 0, (1, 1): 0}
+ROW2, ROW3 = 4, 8
+V_SHARE = {(0, 0): 0, (1, 0): 96, (0, 1): 0, (1, 1): 0}
 GAIN2_ON_SCALAR = [(1, 0), (1, 1), (1, 2), (1, 3)]
 
 
@@ -37,11 +38,11 @@ def tile_list_crew_staffing_score_kernel(
     with ExitStack() as ctx:
         lists = ctx.enter_context(tc.tile_pool(name="lists", bufs=1))
         keep = ctx.enter_context(tc.tile_pool(name="keep", bufs=1))
-        ring = ctx.enter_context(tc.tile_pool(name="ring", bufs=3))
+        ring = ctx.enter_context(tc.tile_pool(name="ring", bufs=4))
         psum = ctx.enter_context(tc.psum_pool(name="psum", bufs=8))
 
         def held(name, shape, dtype):
-            return keep.tile(shape, dtype, name=name, align_bytes=64)
+            return keep.tile(shape, dtype, name=name, tag=name, align_bytes=64)
 
         def load_list(name, src):
             tile = lists.tile([P, 32], U16, name=name)
@@ -67,16 +68,16 @@ def tile_list_crew_staffing_score_kernel(
             return tile
 
         def load_planes_side_by_side(queue, tile, scales):
-            for q in range(QUADS):
+            for r in range(4):
                 queue.dma_start(
-                    tile[32 * q : 32 * q + 4, :].bitcast(I32).rearrange("r (a n) -> r a n", a=PASSES),
-                    scales[:, 4 * q : 4 * q + 4, :].bitcast(I32).rearrange("a r n -> r a n"),
+                    tile[r:P:32, :].bitcast(I32).rearrange("q (a n) -> q a n", a=PASSES),
+                    scales[:, r:16:4, :].bitcast(I32).rearrange("a q n -> q a n"),
                 )
 
-        def load_planes_stacked(queue, tile, scales):
+        def load_planes_stacked(queue, tile, scales, row0):
             for q in range(QUADS):
                 queue.dma_start(
-                    tile[32 * q : 32 * q + 8, :].bitcast(I32),
+                    tile[32 * q + row0 : 32 * q + row0 + 8, :].bitcast(I32),
                     scales[:, 4 * q : 4 * q + 4, :].bitcast(I32),
                 )
 
@@ -111,10 +112,10 @@ def tile_list_crew_staffing_score_kernel(
         idx3 = load_list("idx3", offs3)
         tab3_w = load_both_passes("tab3_w", tab3_words)
         w1_raw = {}
-        load_planes_stacked(nc.sync, tab2_s, tab2_scales)
+        load_planes_stacked(nc.sync, tab2_s, tab2_scales, ROW2)
         w1_raw[0, 0] = load_w1(0, 0)
-        load_planes_stacked(nc.sync, tab3_s, tab3_scales)
         w1_raw[1, 0] = load_w1(1, 0)
+        load_planes_stacked(nc.sync, tab3_s, tab3_scales, ROW3)
         w1_raw[0, 1] = load_w1(0, 1)
         w1_raw[1, 1] = load_w1(1, 1)
         g2 = held("g2", [P, BLOCKS, PACK], F32)
@@ -153,6 +154,7 @@ def tile_list_crew_staffing_score_kernel(
         y2 = {}
 
         def second_product(b):
+            y2_block = keep.tile([P, NJ, JT, PACK], F32, name="y2_%d" % b, tag="w1_raw_10" if b else "y2_0", align_bytes=64)
             for jq in range(NJ):
                 def w4_cols(a, t):
                     c0 = a * H + b * PASS + t * P
@@ -160,8 +162,8 @@ def tile_list_crew_staffing_score_kernel(
 
                 bank = psum.tile([P, PACK, JT], F32, name="ybank")
                 product(bank, w4_cols, v_cols(jq))
-                y2[b, jq] = held("y2_%d%d" % (b, jq), [P, JT, PACK], F32)
-                nc.scalar.copy(y2[b, jq][:], bank[:].rearrange(interleaved))
+                y2[b, jq] = y2_block[:, jq]
+                nc.scalar.copy(y2[b, jq], bank[:].rearrange(interleaved))
 
         second_product(0)
         v2_w = [gather("v2_w%d" % a, tab2_w[a], idx2, U32) for a in range(BLOCKS)]
@@ -184,7 +186,9 @@ def tile_list_crew_staffing_score_kernel(
 
         hq_w, hq_s = {}, {}
 
-        def unit(b, jq):
+        h_bf = {}
+
+        def unit_front(b, jq):
             def w1_cols(a, t):
                 cols = slice(t * P, (t + 1) * P)
                 return w1q_w[a, b][:, cols].bitcast(FP8X4), w1q_s[a, b][:, cols]
@@ -195,6 +199,8 @@ def tile_list_crew_staffing_score_kernel(
             larger = ring.tile([P, JT, PACK], F32, name="larger")
             h = ring.tile([P, 2, JT, PACK], BF16, name="h", align_bytes=64)
             silu = ring.tile([P, PACK * JT], F32, name="silu")
+            nc.vector.tensor_tensor(larger[:], y1, y2[b, jq], ALU.max)
+            h2 = None
             if (b, jq) in GAIN2_ON_SCALAR:
                 h2 = ring.tile([P, PACK, JT], BF16, name="h2")
                 nc.scalar.activation(silu[:], bank[:].rearrange("p t j -> p (t j)"), ACT.Silu)
@@ -203,16 +209,27 @@ def tile_list_crew_staffing_score_kernel(
                         h2[:, t, :], silu[:, t * JT : (t + 1) * JT], ACT.Copy, scale=g2[:, b, t : t + 1]
                     )
             else:
-                silu_jt = silu[:].rearrange("p (j t) -> p j t", t=PACK)
-                nc.scalar.activation(silu_jt, y1, ACT.Silu)
-            nc.vector.tensor_tensor(larger[:], y1, y2[b, jq][:], ALU.max)
-            if (b, jq) not in GAIN2_ON_SCALAR:
-                nc.vector.tensor_tensor(h[:, 0], silu_jt, g2[:, b : b + 1, :].to_broadcast([P, JT, PACK]), ALU.mult)
+                nc.scalar.activation(silu[:].rearrange("p (j t) -> p j t", t=PACK), y1, ACT.Silu)
+            h_bf[b, jq] = (larger, silu, h2, h)
+
+        def unit_gain3(b, jq):
+            larger, silu, h2, h = h_bf[b, jq]
             nc.vector.tensor_tensor(h[:, 1], larger[:], g3[:, b : b + 1, :].to_broadcast([P, JT, PACK]), ALU.mult)
-            if (b, jq) in GAIN2_ON_SCALAR:
+
+        def unit_gain2(b, jq):
+            larger, silu, h2, h = h_bf[b, jq]
+            if h2 is None:
+                nc.vector.tensor_tensor(
+                    h[:, 0], silu[:].rearrange("p (j t) -> p j t", t=PACK),
+                    g2[:, b : b + 1, :].to_broadcast([P, JT, PACK]), ALU.mult,
+                )
+            else:
                 nc.vector.tensor_copy(
                     h[:, 0].rearrange("p (c i) t -> p c t i", i=4), h2[:].rearrange("p t (c i) -> p c t i", i=4)
                 )
+
+        def unit_quantise(b, jq):
+            h = h_bf[b, jq][3]
             hq_w[b, jq] = held("hq_w%d%d" % (b, jq), [P, 2 * JT], U32)
             hq_s[b, jq] = held("hq_s%d%d" % (b, jq), [P, 2 * JT], U8)
             nc.vector.quantize_mx(
@@ -220,10 +237,10 @@ def tile_list_crew_staffing_score_kernel(
             )
 
         def scores(jq):
-            def cand(words, planes):
+            def cand(words, planes, row0):
                 return lambda a, mt: (
                     words[a][:, mt * P : (mt + 1) * P].bitcast(FP8X4),
-                    planes[4 * a : P, mt * P : (mt + 1) * P],
+                    planes[row0 + 4 * a : P, mt * P : (mt + 1) * P],
                 )
 
             def h_cols(e):
@@ -232,8 +249,8 @@ def tile_list_crew_staffing_score_kernel(
 
             e2 = psum.tile([P, MT, JT], F32, name="ybank")
             e3 = psum.tile([P, MT, JT], F32, name="ybank")
-            product(e2, cand(v2_w, v2_s), h_cols(0))
-            product(e3, cand(v3_w, v3_s), h_cols(1))
+            product(e2, cand(v2_w, v2_s, ROW2), h_cols(0))
+            product(e3, cand(v3_w, v3_s, ROW3), h_cols(1))
             th = ring.tile([P, MT, JT], F32, name="th")
             res = ring.tile([P, MT, JT], F32, name="res")
             nc.scalar.activation(th[:], e2[:], ACT.Tanh)
@@ -245,15 +262,21 @@ def tile_list_crew_staffing_score_kernel(
 
         for a in range(PASSES):
             quantise_w1(a, 0)
-        second_product(1)
         v3_w = [gather("v3_w%d" % a, tab3_w[a], idx3, U32) for a in range(BLOCKS)]
         v3_s = gather("v3_s", tab3_s[:], idx3, U8)
-        for jq in range(NJ):
-            unit(0, jq)
-            if jq % 2 == 1:
-                quantise_w1(jq // 2, 1)
-        for jq in range(NJ):
-            unit(1, jq)
-            if jq > 0:
-                scores(jq - 1)
-        scores(NJ - 1)
+        units = [(b, jq) for b in range(BLOCKS) for jq in range(NJ)]
+        for n in range(len(units) + 2):
+            if n < len(units):
+                unit_front(*units[n])
+            if n == 0:
+                second_product(1)
+            if 1 <= n <= len(units):
+                unit_gain2(*units[n - 1])
+            if n in (2, 3):
+                quantise_w1(n - 2, 1)
+            if n < len(units):
+                unit_gain3(*units[n])
+            if n >= NJ + 2:
+                scores(n - NJ - 2)
+            if 1 <= n <= len(units):
+                unit_quantise(*units[n - 1])

@@ -26,7 +26,6 @@ NJ = S // JT
 MT = S2 // P
 QUADS = 4
 ROW2, ROW3 = 4, 8
-V_SHARE = {(0, 0): 0, (1, 0): 96, (0, 1): 0, (1, 1): 0}
 GAIN2_ON_SCALAR = [(1, 0), (1, 1), (1, 2), (1, 3)]
 
 
@@ -173,13 +172,13 @@ def tile_list_crew_staffing_score_kernel(
 
         def quantise_w1(a, b):
             grouped = held("w1_bf_%d%d" % (a, b), [P, PASS * PACK], BF16)
-            dst = grouped[:].rearrange("p (t m i) -> p m i t", t=PACK, i=PACK)
-            src = w1_raw[a, b][:].rearrange("p i (m t) -> p m i t", t=PACK)
-            cut = V_SHARE[a, b]
-            if cut > 0:
-                nc.vector.tensor_copy(dst[:, :cut], src[:, :cut])
-            if cut < P:
-                nc.scalar.copy(dst[:, cut:], src[:, cut:])
+            dst = grouped[:].rearrange("p (u e m i) -> p u m i e", u=2, e=2, i=PACK)
+            src = w1_raw[a, b][:].rearrange("p i (m u e) -> p u m i e", u=2, e=2)
+            for u in range(2):
+                if (a, b, u) == (1, 0, 0):
+                    nc.vector.tensor_copy(dst[:, u], src[:, u])
+                else:
+                    nc.scalar.copy(dst[:, u], src[:, u])
             w1q_w[a, b] = held("w1q_w%d%d" % (a, b), [P, PASS], U32)
             w1q_s[a, b] = held("w1q_s%d%d" % (a, b), [P, PASS], U8)
             nc.vector.quantize_mx(w1q_w[a, b][:].bitcast(FP8X4), w1q_s[a, b][:], grouped[:])

@@ -26,7 +26,7 @@ NJ = S // JT
 MT = S2 // P
 QUADS = 4
 ROW2, ROW3 = 4, 8
-GAIN2_ON_SCALAR = [(1, 0), (1, 1), (1, 2), (1, 3)]
+JH = 2 * JT
 
 
 def tile_list_crew_staffing_score_kernel(
@@ -108,22 +108,21 @@ def tile_list_crew_staffing_score_kernel(
         load_planes_side_by_side(nc.sync, w4_s, w4_scales)
         idx2 = load_list("idx2", offs2)
         tab2_w = load_both_passes("tab2_w", tab2_words)
+        load_planes_stacked(nc.sync, tab2_s, tab2_scales, ROW2)
+        w1_raw = {}
+        w1_raw[0, 0] = load_w1(0, 0)
         idx3 = load_list("idx3", offs3)
         tab3_w = load_both_passes("tab3_w", tab3_words)
-        w1_raw = {}
-        load_planes_stacked(nc.sync, tab2_s, tab2_scales, ROW2)
-        w1_raw[0, 0] = load_w1(0, 0)
         w1_raw[1, 0] = load_w1(1, 0)
         load_planes_stacked(nc.sync, tab3_s, tab3_scales, ROW3)
+        gains = held("gains", [P, 2, BLOCKS, PACK], F32)
+        d_sb = held("d_sb", [P, MT], F32)
+        nc.sync.dma_start(gains[:, 0], gain2.rearrange("(b p t) -> p b t", p=P, t=PACK))
+        nc.sync.dma_start(gains[:, 1], gain3.rearrange("(b p t) -> p b t", p=P, t=PACK))
         w1_raw[0, 1] = load_w1(0, 1)
         w1_raw[1, 1] = load_w1(1, 1)
-        g2 = held("g2", [P, BLOCKS, PACK], F32)
-        g3 = held("g3", [P, BLOCKS, PACK], F32)
-        d_sb = held("d_sb", [P, MT], F32)
-        nc.gpsimd.dma_start(g2[:], gain2.rearrange("(b p t) -> p b t", p=P, t=PACK))
-        nc.gpsimd.dma_start(g3[:], gain3.rearrange("(b p t) -> p b t", p=P, t=PACK))
         with nc.allow_non_contiguous_dma(reason="one value of d for each partition and row tile"):
-            nc.gpsimd.dma_start(d_sb[:], d.rearrange("(mt p) -> p mt", p=P))
+            nc.sync.dma_start(d_sb[:], d.rearrange("(mt p) -> p mt", p=P))
 
         v_w = [gather("v_w0", tab_w[0][:], idx, U32)]
         v_s = [gather("v_s%d" % a, tab_s[:, a * T : (a + 1) * T], idx, U8) for a in range(PASSES)]
@@ -134,8 +133,8 @@ def tile_list_crew_staffing_score_kernel(
         nc.vector.tensor_copy(w4q_s[:].rearrange(deal_out, t=PACK, m=P), w4_s[:].rearrange(deal_in, t=PACK, m=P))
         v_w.append(gather("v_w1", tab_w[1][:], idx, U32))
 
-        def product(bank, lhs, rhs):
-            for a in range(2):
+        def product(bank, lhs, rhs, passes):
+            for a in passes:
                 for t in range(4):
                     lw, ls = lhs(a, t)
                     rw, rs = rhs(a)
@@ -153,18 +152,19 @@ def tile_list_crew_staffing_score_kernel(
         y2 = {}
 
         def second_product(b):
-            y2_block = keep.tile([P, NJ, JT, PACK], F32, name="y2_%d" % b, tag="w1_raw_10" if b else "y2_0", align_bytes=64)
+            y2_block = keep.tile([P, NJ, JT, PACK], F32, name="y2_%d" % b)
             for jq in range(NJ):
                 def w4_cols(a, t):
                     c0 = a * H + b * PASS + t * P
                     return w4q_w[:, c0 : c0 + P].bitcast(FP4X4), w4q_s[:, c0 : c0 + P]
 
                 bank = psum.tile([P, PACK, JT], F32, name="ybank")
-                product(bank, w4_cols, v_cols(jq))
+                product(bank, w4_cols, v_cols(jq), (0, 1))
                 y2[b, jq] = y2_block[:, jq]
                 nc.scalar.copy(y2[b, jq], bank[:].rearrange(interleaved))
 
         second_product(0)
+        second_product(1)
         v2_w = [gather("v2_w%d" % a, tab2_w[a], idx2, U32) for a in range(BLOCKS)]
         v2_s = gather("v2_s", tab2_s[:], idx2, U8)
 
@@ -175,7 +175,7 @@ def tile_list_crew_staffing_score_kernel(
             dst = grouped[:].rearrange("p (u e m i) -> p u m i e", u=2, e=2, i=PACK)
             src = w1_raw[a, b][:].rearrange("p i (m u e) -> p u m i e", u=2, e=2)
             for u in range(2):
-                if (a, b, u) == (1, 0, 0):
+                if (a, b) == (0, 0) or (a, u) == (1, 0):
                     nc.vector.tensor_copy(dst[:, u], src[:, u])
                 else:
                     nc.scalar.copy(dst[:, u], src[:, u])
@@ -183,99 +183,114 @@ def tile_list_crew_staffing_score_kernel(
             w1q_s[a, b] = held("w1q_s%d%d" % (a, b), [P, PASS], U8)
             nc.vector.quantize_mx(w1q_w[a, b][:].bitcast(FP8X4), w1q_s[a, b][:], grouped[:])
 
-        hq_w, hq_s = {}, {}
+        hq_w, hq_s, pre, h_bf = {}, {}, {}, {}
 
-        h_bf = {}
+        y1_bank = {}
 
-        def unit_front(b, jq):
+        def first_products(b):
             def w1_cols(a, t):
                 cols = slice(t * P, (t + 1) * P)
                 return w1q_w[a, b][:, cols].bitcast(FP8X4), w1q_s[a, b][:, cols]
 
-            bank = psum.tile([P, PACK, JT], F32, name="ybank")
-            product(bank, w1_cols, v_cols(jq))
+            for jq in range(NJ):
+                y1_bank[b, jq] = psum.tile([P, PACK, JT], F32, name="ybank")
+            for a in range(PASSES):
+                for jq in range(NJ):
+                    product(y1_bank[b, jq], w1_cols, v_cols(jq), (a,))
+
+        def first_product(b, jq):
+            half, cols = jq // 2, slice(jq % 2 * JT, (jq % 2 + 1) * JT)
+            if jq % 2 == 0:
+                pre[b, half] = ring.tile([P, 2, JH * PACK], F32, name="pre")
+            bank = y1_bank[b, jq]
             y1 = bank[:].rearrange(interleaved)
-            larger = ring.tile([P, JT, PACK], F32, name="larger")
-            h = ring.tile([P, 2, JT, PACK], BF16, name="h", align_bytes=64)
-            silu = ring.tile([P, PACK * JT], F32, name="silu")
-            nc.vector.tensor_tensor(larger[:], y1, y2[b, jq], ALU.max)
-            h2 = None
-            if (b, jq) in GAIN2_ON_SCALAR:
-                h2 = ring.tile([P, PACK, JT], BF16, name="h2")
-                nc.scalar.activation(silu[:], bank[:].rearrange("p t j -> p (t j)"), ACT.Silu)
+            both = pre[b, half][:].rearrange("p e (j t) -> p e j t", t=PACK)
+            if b == 0:
+                nc.scalar.activation(both[:, 0, cols], y1, ACT.Silu)
+            else:
+                silu = pre[b, half][:, 0].rearrange("p (t j) -> p t j", t=PACK)
+                nc.scalar.activation(silu[:, :, cols], bank[:], ACT.Silu)
+            nc.vector.tensor_tensor(both[:, 1, cols], y1, y2[b, jq], ALU.max)
+
+        def apply_gains(b, half):
+            h = ring.tile([P, 2, JH, PACK], BF16, name="h", align_bytes=64)
+            h_bf[b, half] = h
+            both = pre[b, half][:].rearrange("p e (j t) -> p e j t", t=PACK)
+            spread = gains[:, :, b : b + 1, :].to_broadcast([P, 2, JH, PACK])
+            if b == 0:
+                for e in range(2):
+                    nc.vector.tensor_tensor(h[:, e], both[:, e], spread[:, e], ALU.mult)
+            else:
+                h2 = ring.tile([P, PACK, JH], BF16, name="h2")
                 for t in range(PACK):
                     nc.scalar.activation(
-                        h2[:, t, :], silu[:, t * JT : (t + 1) * JT], ACT.Copy, scale=g2[:, b, t : t + 1]
+                        h2[:, t, :], pre[b, half][:, 0, t * JH : (t + 1) * JH], ACT.Copy,
+                        scale=gains[:, 0, b, t : t + 1],
                     )
-            else:
-                nc.scalar.activation(silu[:].rearrange("p (j t) -> p j t", t=PACK), y1, ACT.Silu)
-            h_bf[b, jq] = (larger, silu, h2, h)
-
-        def unit_gain3(b, jq):
-            larger, silu, h2, h = h_bf[b, jq]
-            nc.vector.tensor_tensor(h[:, 1], larger[:], g3[:, b : b + 1, :].to_broadcast([P, JT, PACK]), ALU.mult)
-
-        def unit_gain2(b, jq):
-            larger, silu, h2, h = h_bf[b, jq]
-            if h2 is None:
-                nc.vector.tensor_tensor(
-                    h[:, 0], silu[:].rearrange("p (j t) -> p j t", t=PACK),
-                    g2[:, b : b + 1, :].to_broadcast([P, JT, PACK]), ALU.mult,
-                )
-            else:
+                nc.vector.tensor_tensor(h[:, 1], both[:, 1], spread[:, 1], ALU.mult)
                 nc.vector.tensor_copy(
                     h[:, 0].rearrange("p (c i) t -> p c t i", i=4), h2[:].rearrange("p t (c i) -> p c t i", i=4)
                 )
 
-        def unit_quantise(b, jq):
-            h = h_bf[b, jq][3]
-            hq_w[b, jq] = held("hq_w%d%d" % (b, jq), [P, 2 * JT], U32)
-            hq_s[b, jq] = held("hq_s%d%d" % (b, jq), [P, 2 * JT], U8)
+        def quantise_h(b, half):
+            hq_w[b, half] = held("hq_w%d%d" % (b, half), [P, 2 * JH], U32)
+            hq_s[b, half] = held("hq_s%d%d" % (b, half), [P, 2 * JH], U8)
             nc.vector.quantize_mx(
-                hq_w[b, jq][:].bitcast(FP8X4), hq_s[b, jq][:], h[:].rearrange("p e j t -> p (e j t)")
+                hq_w[b, half][:].bitcast(FP8X4), hq_s[b, half][:], h_bf[b, half][:].rearrange("p e j t -> p (e j t)")
             )
 
-        def scores(jq):
-            def cand(words, planes, row0):
-                return lambda a, mt: (
-                    words[a][:, mt * P : (mt + 1) * P].bitcast(FP8X4),
-                    planes[row0 + 4 * a : P, mt * P : (mt + 1) * P],
-                )
+        score_parts = {}
 
-            def h_cols(e):
-                cols = slice(e * JT, (e + 1) * JT)
-                return lambda a: (hq_w[a, jq][:, cols].bitcast(FP8X4), hq_s[a, jq][:, cols])
+        def score_products(half):
+            banks = [[psum.tile([P, 2, JH], F32, name="ybank") for e in range(2)] for pair in range(2)]
+            for b in range(BLOCKS):
+                for pair in range(2):
+                    for e, (words, planes, row0) in enumerate(((v2_w, v2_s, ROW2), (v3_w, v3_s, ROW3))):
+                        for s in range(2):
+                            crews = slice((2 * pair + s) * P, (2 * pair + s + 1) * P)
+                            cols = slice(e * JH, (e + 1) * JH)
+                            nc.tensor.matmul_mx(
+                                out=banks[pair][e][:, s, :],
+                                lhsT=words[b][:, crews].bitcast(FP8X4), lhsT_scale=planes[row0 + 4 * b : P, crews],
+                                rhs=hq_w[b, half][:, cols].bitcast(FP8X4), rhs_scale=hq_s[b, half][:, cols],
+                                start=(b == 0 and s == 0), stop=(b == BLOCKS - 1 and s == 1),
+                            )
+            for pair in range(2):
+                th = ring.tile([P, 2, JH], F32, name="th")
+                nc.scalar.activation(th[:], banks[pair][0][:], ACT.Tanh)
+                score_parts[half, pair] = (banks[pair][1], th)
 
-            e2 = psum.tile([P, MT, JT], F32, name="ybank")
-            e3 = psum.tile([P, MT, JT], F32, name="ybank")
-            product(e2, cand(v2_w, v2_s, ROW2), h_cols(0))
-            product(e3, cand(v3_w, v3_s, ROW3), h_cols(1))
-            th = ring.tile([P, MT, JT], F32, name="th")
-            res = ring.tile([P, MT, JT], F32, name="res")
-            nc.scalar.activation(th[:], e2[:], ACT.Tanh)
-            for mt in range(MT):
-                nc.vector.scalar_tensor_tensor(
-                    res[:, mt, :], e3[:, mt, :], d_sb[:, mt : mt + 1], th[:, mt, :], ALU.add, ALU.mult
-                )
-            nc.sync.dma_start(out[:, jq * JT : (jq + 1) * JT].rearrange("(mt p) j -> p mt j", p=P), res[:])
+        def score_out(half):
+            out_cols = out[:, half * JH : (half + 1) * JH].rearrange("(mt p) j -> p mt j", p=P)
+            for pair in range(2):
+                e3, th = score_parts[half, pair]
+                res = ring.tile([P, 2, JH], F32, name="res")
+                for s in range(2):
+                    mt = 2 * pair + s
+                    nc.vector.scalar_tensor_tensor(
+                        res[:, s, :], e3[:, s, :], d_sb[:, mt : mt + 1], th[:, s, :], ALU.add, ALU.mult
+                    )
+                nc.sync.dma_start(out_cols[:, 2 * pair : 2 * pair + 2, :], res[:])
 
-        for a in range(PASSES):
-            quantise_w1(a, 0)
+        quantise_w1(0, 0)
         v3_w = [gather("v3_w%d" % a, tab3_w[a], idx3, U32) for a in range(BLOCKS)]
+        quantise_w1(1, 0)
         v3_s = gather("v3_s", tab3_s[:], idx3, U8)
-        units = [(b, jq) for b in range(BLOCKS) for jq in range(NJ)]
-        for n in range(len(units) + 2):
-            if n < len(units):
-                unit_front(*units[n])
-            if n == 0:
-                second_product(1)
-            if 1 <= n <= len(units):
-                unit_gain2(*units[n - 1])
-            if n in (2, 3):
-                quantise_w1(n - 2, 1)
-            if n < len(units):
-                unit_gain3(*units[n])
-            if n >= NJ + 2:
-                scores(n - NJ - 2)
-            if 1 <= n <= len(units):
-                unit_quantise(*units[n - 1])
+        for b in range(BLOCKS):
+            first_products(b)
+            first_product(b, 0)
+            first_product(b, 1)
+            first_product(b, 2)
+            apply_gains(b, 0)
+            first_product(b, 3)
+            if b == 0:
+                for a in range(PASSES):
+                    quantise_w1(a, 1)
+            quantise_h(b, 0)
+            if b == 1:
+                score_products(0)
+            apply_gains(b, 1)
+            quantise_h(b, 1)
+        score_products(1)
+        score_out(0)
+        score_out(1)

from contextlib import ExitStack

import concourse.mybir as mybir

K, T, S, H, T3, S2 = 1024, 2048, 512, 1024, 1024, 512
FLOPS = 2 * (2 * K * H * S + 2 * H * S2 * S)

F32 = mybir.dt.float32
BF16 = mybir.dt.bfloat16
I32 = mybir.dt.int32
U32 = mybir.dt.uint32
U16 = mybir.dt.uint16
U8 = mybir.dt.uint8
FP8X4 = mybir.dt.float8_e4m3fn_x4
FP4X4 = mybir.dt.float4_e2m1fn_x4
ACT = mybir.ActivationFunctionType
ALU = mybir.AluOpType

P = 128
PACK = 4
PASS = P * PACK
PASSES = K // PASS
BLOCKS = H // PASS
JT = 128
NJ = S // JT
MT = S2 // P
QUADS = 4
ROW2, ROW3 = 4, 8
JH = 2 * JT


def tile_list_crew_staffing_score_kernel(
    tc, tab_words, tab_scales, offs, tab2_words, tab2_scales, offs2, tab3_words, tab3_scales, offs3,
    w1, w4_words, w4_scales, gain2, gain3, d, out,
):
    nc = tc.nc
    with ExitStack() as ctx:
        lists = ctx.enter_context(tc.tile_pool(name="lists", bufs=1))
        keep = ctx.enter_context(tc.tile_pool(name="keep", bufs=1))
        ring = ctx.enter_context(tc.tile_pool(name="ring", bufs=4))
        psum = ctx.enter_context(tc.psum_pool(name="psum", bufs=8))

        def held(name, shape, dtype):
            return keep.tile(shape, dtype, name=name, tag=name, align_bytes=64)

        def load_list(name, src):
            tile = lists.tile([P, 32], U16, name=name)
            nc.sync.dma_start(tile[:], src)
            return tile

        def load_words(name, src, cols):
            tile = held(name, [P, cols], U32)
            nc.sync.dma_start(tile[:].bitcast(I32), src.rearrange("p n i -> p (n i)").bitcast(I32))
            return tile

        def load_both_passes(name, src):
            tile = held(name, [P, BLOCKS * T3], U32)
            nc.sync.dma_start(
                tile[:].bitcast(I32).rearrange("p (a n) -> p a n", a=BLOCKS),
                src.rearrange("a p n i -> p a (n i)").bitcast(I32),
            )
            return [tile[:, a * T3 : (a + 1) * T3] for a in range(BLOCKS)]

        def zeroed_bytes(engine, name, cols):
            tile = held(name, [P, cols], U8)
            engine.memset(tile[:].bitcast(I32), 0)
            return tile

        def load_planes_side_by_side(queue, tile, scales):
            for r in range(4):
                queue.dma_start(
                    tile[r:P:32, :].bitcast(I32).rearrange("q (a n) -> q a n", a=PASSES),
                    scales[:, r:16:4, :].bitcast(I32).rearrange("a q n -> q a n"),
                )

        def load_planes_stacked(queue, tile, scales, row0):
            for q in range(QUADS):
                queue.dma_start(
                    tile[32 * q + row0 : 32 * q + row0 + 8, :].bitcast(I32),
                    scales[:, 4 * q : 4 * q + 4, :].bitcast(I32),
                )

        def gather(name, window, offsets, dtype):
            tile = held(name, [P, S], dtype)
            nc.vector.tensor_copy(tile[:], window.indirect(offsets[:]))
            return tile

        def load_w1(a, b):
            tile = held("w1_raw_%d%d" % (a, b), [P, PACK, PASS], F32)
            rows = w1[a * PASS : (a + 1) * PASS, b * PASS : (b + 1) * PASS]
            nc.sync.dma_start(tile[:], rows.rearrange("(p i) c -> p i c", i=PACK))
            return tile

        tab_s = zeroed_bytes(nc.vector, "tab_s", PASSES * T)
        w4_s = zeroed_bytes(nc.vector, "w4_s", PASSES * H)
        tab2_s = zeroed_bytes(nc.vector, "tab2_s", T3)
        tab3_s = zeroed_bytes(nc.vector, "tab3_s", T3)

        idx = load_list("idx", offs)
        tab_w = [load_words("tab_w0", tab_words[0], T)]
        load_planes_side_by_side(nc.sync, tab_s, tab_scales)
        w4_w = held("w4_w", [P, PASSES * H], U16)
        nc.sync.dma_start(
            w4_w[:].bitcast(I32).rearrange("p (a n) -> p a n", a=PASSES),
            w4_words.bitcast(I32).rearrange("a p n -> p a n"),
        )
        tab_w.append(load_words("tab_w1", tab_words[1], T))
        load_planes_side_by_side(nc.sync, w4_s, w4_scales)
        idx2 = load_list("idx2", offs2)
        tab2_w = load_both_passes("tab2_w", tab2_words)
        load_planes_stacked(nc.sync, tab2_s, tab2_scales, ROW2)
        w1_raw = {}
        w1_raw[0, 0] = load_w1(0, 0)
        idx3 = load_list("idx3", offs3)
        tab3_w = load_both_passes("tab3_w", tab3_words)
        w1_raw[1, 0] = load_w1(1, 0)
        load_planes_stacked(nc.sync, tab3_s, tab3_scales, ROW3)
        gains = held("gains", [P, 2, BLOCKS, PACK], F32)
        d_sb = held("d_sb", [P, MT], F32)
        nc.sync.dma_start(gains[:, 0], gain2.rearrange("(b p t) -> p b t", p=P, t=PACK))
        nc.sync.dma_start(gains[:, 1], gain3.rearrange("(b p t) -> p b t", p=P, t=PACK))
        w1_raw[0, 1] = load_w1(0, 1)
        w1_raw[1, 1] = load_w1(1, 1)
        with nc.allow_non_contiguous_dma(reason="one value of d for each partition and row tile"):
            nc.sync.dma_start(d_sb[:], d.rearrange("(mt p) -> p mt", p=P))

        v_w = [gather("v_w0", tab_w[0][:], idx, U32)]
        v_s = [gather("v_s%d" % a, tab_s[:, a * T : (a + 1) * T], idx, U8) for a in range(PASSES)]
        w4q_w = held("w4q_w", [P, PASSES * H], U16)
        w4q_s = held("w4q_s", [P, PASSES * H], U8)
        deal_out, deal_in = "p (g t m) -> p g t m", "p (g m t) -> p g t m"
        nc.scalar.copy(w4q_w[:].rearrange(deal_out, t=PACK, m=P), w4_w[:].rearrange(deal_in, t=PACK, m=P))
        nc.vector.tensor_copy(w4q_s[:].rearrange(deal_out, t=PACK, m=P), w4_s[:].rearrange(deal_in, t=PACK, m=P))
        v_w.append(gather("v_w1", tab_w[1][:], idx, U32))

        def product(bank, lhs, rhs, passes):
            for a in passes:
                for t in range(4):
                    lw, ls = lhs(a, t)
                    rw, rs = rhs(a)
                    nc.tensor.matmul_mx(
                        out=bank[:, t, :], lhsT=lw, lhsT_scale=ls, rhs=rw, rhs_scale=rs,
                        start=(a == 0 and t == 0), stop=(a == 1 and t == 3),
                    )

        def v_cols(jq):
            cols = slice(jq * JT, (jq + 1) * JT)
            return lambda a: (v_w[a][:, cols].bitcast(FP8X4), v_s[a][:, cols])

        interleaved = "p t j -> p j t"

        y2 = {}

        def second_product(b):
            y2_block = keep.tile([P, NJ, JT, PACK], F32, name="y2_%d" % b)
            for jq in range(NJ):
                def w4_cols(a, t):
                    c0 = a * H + b * PASS + t * P
                    return w4q_w[:, c0 : c0 + P].bitcast(FP4X4), w4q_s[:, c0 : c0 + P]

                bank = psum.tile([P, PACK, JT], F32, name="ybank")
                product(bank, w4_cols, v_cols(jq), (0, 1))
                y2[b, jq] = y2_block[:, jq]
                nc.scalar.copy(y2[b, jq], bank[:].rearrange(interleaved))

        second_product(0)
        second_product(1)
        v2_w = [gather("v2_w%d" % a, tab2_w[a], idx2, U32) for a in range(BLOCKS)]
        v2_s = gather("v2_s", tab2_s[:], idx2, U8)

        w1q_w, w1q_s = {}, {}

        def quantise_w1(a, b):
            grouped = held("w1_bf_%d%d" % (a, b), [P, PASS * PACK], BF16)
            dst = grouped[:].rearrange("p (u e m i) -> p u m i e", u=2, e=2, i=PACK)
            src = w1_raw[a, b][:].rearrange("p i (m u e) -> p u m i e", u=2, e=2)
            for u in range(2):
                if (a, b) == (0, 0) or (a, u) == (1, 0):
                    nc.vector.tensor_copy(dst[:, u], src[:, u])
                else:
                    nc.scalar.copy(dst[:, u], src[:, u])
            w1q_w[a, b] = held("w1q_w%d%d" % (a, b), [P, PASS], U32)
            w1q_s[a, b] = held("w1q_s%d%d" % (a, b), [P, PASS], U8)
            nc.vector.quantize_mx(w1q_w[a, b][:].bitcast(FP8X4), w1q_s[a, b][:], grouped[:])

        hq_w, hq_s, pre, h_bf = {}, {}, {}, {}

        y1_bank = {}

        def first_products(b):
            def w1_cols(a, t):
                cols = slice(t * P, (t + 1) * P)
                return w1q_w[a, b][:, cols].bitcast(FP8X4), w1q_s[a, b][:, cols]

            for jq in range(NJ):
                y1_bank[b, jq] = psum.tile([P, PACK, JT], F32, name="ybank")
            for a in range(PASSES):
                for jq in range(NJ):
                    product(y1_bank[b, jq], w1_cols, v_cols(jq), (a,))

        def first_product(b, jq):
            half, cols = jq // 2, slice(jq % 2 * JT, (jq % 2 + 1) * JT)
            if jq % 2 == 0:
                pre[b, half] = ring.tile([P, 2, JH * PACK], F32, name="pre")
            bank = y1_bank[b, jq]
            y1 = bank[:].rearrange(interleaved)
            both = pre[b, half][:].rearrange("p e (j t) -> p e j t", t=PACK)
            if b == 0:
                nc.scalar.activation(both[:, 0, cols], y1, ACT.Silu)
            else:
                silu = pre[b, half][:, 0].rearrange("p (t j) -> p t j", t=PACK)
                nc.scalar.activation(silu[:, :, cols], bank[:], ACT.Silu)
            nc.vector.tensor_tensor(both[:, 1, cols], y1, y2[b, jq], ALU.max)

        def apply_gains(b, half):
            h = ring.tile([P, 2, JH, PACK], BF16, name="h", align_bytes=64)
            h_bf[b, half] = h
            both = pre[b, half][:].rearrange("p e (j t) -> p e j t", t=PACK)
            spread = gains[:, :, b : b + 1, :].to_broadcast([P, 2, JH, PACK])
            if b == 0:
                for e in range(2):
                    nc.vector.tensor_tensor(h[:, e], both[:, e], spread[:, e], ALU.mult)
            else:
                h2 = ring.tile([P, PACK, JH], BF16, name="h2")
                for t in range(PACK):
                    nc.scalar.activation(
                        h2[:, t, :], pre[b, half][:, 0, t * JH : (t + 1) * JH], ACT.Copy,
                        scale=gains[:, 0, b, t : t + 1],
                    )
                nc.vector.tensor_tensor(h[:, 1], both[:, 1], spread[:, 1], ALU.mult)
                nc.vector.tensor_copy(
                    h[:, 0].rearrange("p (c i) t -> p c t i", i=4), h2[:].rearrange("p t (c i) -> p c t i", i=4)
                )

        def quantise_h(b, half):
            hq_w[b, half] = held("hq_w%d%d" % (b, half), [P, 2 * JH], U32)
            hq_s[b, half] = held("hq_s%d%d" % (b, half), [P, 2 * JH], U8)
            nc.vector.quantize_mx(
                hq_w[b, half][:].bitcast(FP8X4), hq_s[b, half][:], h_bf[b, half][:].rearrange("p e j t -> p (e j t)")
            )

        score_parts = {}

        def score_products(half):
            banks = [[psum.tile([P, 2, JH], F32, name="ybank") for e in range(2)] for pair in range(2)]
            for b in range(BLOCKS):
                for pair in range(2):
                    for e, (words, planes, row0) in enumerate(((v2_w, v2_s, ROW2), (v3_w, v3_s, ROW3))):
                        for s in range(2):
                            crews = slice((2 * pair + s) * P, (2 * pair + s + 1) * P)
                            cols = slice(e * JH, (e + 1) * JH)
                            nc.tensor.matmul_mx(
                                out=banks[pair][e][:, s, :],
                                lhsT=words[b][:, crews].bitcast(FP8X4), lhsT_scale=planes[row0 + 4 * b : P, crews],
                                rhs=hq_w[b, half][:, cols].bitcast(FP8X4), rhs_scale=hq_s[b, half][:, cols],
                                start=(b == 0 and s == 0), stop=(b == BLOCKS - 1 and s == 1),
                            )
            for pair in range(2):
                th = ring.tile([P, 2, JH], F32, name="th")
                nc.scalar.activation(th[:], banks[pair][0][:], ACT.Tanh)
                score_parts[half, pair] = (banks[pair][1], th)

        def score_out(half):
            out_cols = out[:, half * JH : (half + 1) * JH].rearrange("(mt p) j -> p mt j", p=P)
            for pair in range(2):
                e3, th = score_parts[half, pair]
                res = ring.tile([P, 2, JH], F32, name="res")
                for s in range(2):
                    mt = 2 * pair + s
                    nc.vector.scalar_tensor_tensor(
                        res[:, s, :], e3[:, s, :], d_sb[:, mt : mt + 1], th[:, s, :], ALU.add, ALU.mult
                    )
                nc.sync.dma_start(out_cols[:, 2 * pair : 2 * pair + 2, :], res[:])

        quantise_w1(0, 0)
        v3_w = [gather("v3_w%d" % a, tab3_w[a], idx3, U32) for a in range(BLOCKS)]
        quantise_w1(1, 0)
        v3_s = gather("v3_s", tab3_s[:], idx3, U8)
        for b in range(BLOCKS):
            first_products(b)
            first_product(b, 0)
            first_product(b, 1)
            first_product(b, 2)
            apply_gains(b, 0)
            first_product(b, 3)
            if b == 0:
                for a in range(PASSES):
                    quantise_w1(a, 1)
            quantise_h(b, 0)
            if b == 1:
                score_products(0)
            apply_gains(b, 1)
            quantise_h(b, 1)
        score_products(1)
        score_out(0)
        score_out(1)
